import numpy as np
import ml_dtypes


def mxq(x, axis, fmt="e4m3"):
    dtype, down = {"e4m3": (ml_dtypes.float8_e4m3fn, 7), "e5m2": (ml_dtypes.float8_e5m2, 14)}[fmt]
    v = np.moveaxis(np.asarray(x, np.float32).astype(ml_dtypes.bfloat16).astype(np.float64), axis, -1)
    blocks = v.reshape(v.shape[:-1] + (-1, 32))
    amax = np.abs(blocks).max(-1, keepdims=True)
    byte = np.maximum(np.where(amax > 0, np.frexp(amax)[1] - 1 + 127, 0) - down, 1)
    scale = np.exp2(byte - 127.0)
    codes = (blocks / scale).astype(np.float32).astype(dtype).astype(np.float64)
    return np.moveaxis((codes * scale).reshape(v.shape), -1, axis)


WIDE = False


def mx_kscale(k):
    if not WIDE:
        return np.ones(k)
    levels = np.array([10, -10, 5, -5, 0])
    if k % 512:
        return np.exp2(np.random.permutation(np.resize(levels, k // 32))).repeat(32)
    a = np.empty((k // 512, 16))
    for p in range(k // 512):
        a[p, :8] = np.random.permutation(np.resize(levels, 8))
        for g in range(8):
            far = levels[np.abs(levels - a[p, g]) >= 10]
            a[p, g + 8] = far[np.random.randint(len(far))]
    return np.exp2(a.ravel()).repeat(32)


def f64(x):
    return np.asarray(x).astype(np.float64)


def striped(idx):
    return np.tile(idx.reshape(-1, 16).T, (8, 1)).astype(np.uint16)


def unstriped(offs):
    return offs[:16].T.reshape(-1).astype(np.int64)


def striped8(idx):
    return np.concatenate([x.reshape(-1, 16).T for x in idx]).astype(np.uint16)


def runs(offs, k):
    lists = np.stack([offs[16 * r : 16 * r + 16].T.reshape(-1) for r in range(8)]).astype(np.int64)
    return lists[np.arange(k) % 512 // 64]


def pack_weight(w):
    k, n = w.shape
    w = f64(np.asarray(w, np.float32).astype(ml_dtypes.bfloat16)).reshape(k // 32, 32, n)
    amax = np.abs(w).max(1)
    byte = np.clip(np.where(amax > 0, np.frexp(amax)[1] - 1 + 127 - 7, 1), 1, 254)
    scaled = (w * np.exp2(127.0 - byte)[:, None, :]).reshape(k, n).astype(np.float32)
    words = np.ascontiguousarray(scaled.reshape(k // 512, 128, 4, n).transpose(0, 1, 3, 2)).astype(ml_dtypes.float8_e4m3fn).view(np.uint8)
    return words, np.ascontiguousarray(byte.astype(np.uint8).reshape(k // 512, 16, n))


def unpack_weight(words, scales):
    g, p, n, _ = words.shape
    vals = np.ascontiguousarray(words).view(ml_dtypes.float8_e4m3fn).astype(np.float64) * np.repeat(np.exp2(scales.astype(np.float64) - 127.0), 8, axis=1)[..., None]
    return vals.transpose(0, 1, 3, 2).reshape(g * 512, n)

def planes(y):
    n, m = y.shape
    v = y.astype(np.float32).astype(ml_dtypes.bfloat16).astype(np.float64).reshape(n // 32, 32, m)
    top = np.abs(v).max(1)
    byte = np.clip(np.where(top > 0, np.frexp(top)[1] - 1 + 127 - 7, 1), 1, 254)
    codes = (v * np.exp2(127.0 - byte)[:, None, :]).reshape(n, m).astype(np.float32).astype(ml_dtypes.float8_e4m3fn).view(np.uint8)
    words = codes.reshape(n // 512, 128, 4, m).transpose(0, 1, 3, 2)
    return np.ascontiguousarray(words), np.ascontiguousarray(byte.astype(np.uint8).reshape(n // 512, 16, m))


K, T, S, V, N, U, H = 512, 2048, 512, 1024, 512, 1024, 512


def setup_inputs():
    n = np.random.standard_normal
    s = mx_kscale(K)[:, None]
    u = mx_kscale(H)
    packed_xT = pack_weight(n((K, T)) * s)
    packed_w2 = pack_weight(n((H, N)) / np.sqrt(H) / u[:, None])
    return {
        "x_words": packed_xT[0],
        "x_scales": packed_xT[1],
        "w1": (n((K, H)) / np.sqrt(K) / s * u).astype(np.float32),
        "mem": (n((H, U)) * u[:, None]).astype(np.float32),
        "w2_words": packed_w2[0],
        "w2_scales": packed_w2[1],
        "offs": striped(np.random.permutation(T)[:S]),
        "slot": striped8(np.stack([np.random.permutation(U)[:S] for _ in range(8)])),
        "r1": striped8(np.stack([np.random.permutation(U) for _ in range(8)])),
        "r2": striped8(np.stack([np.random.permutation(U) for _ in range(8)])),
    }


def reference(x_words, x_scales, w1, mem, w2_words, w2_scales, offs, slot, r1, r2):
    xq = unpack_weight(x_words, x_scales)[:, unstriped(offs)]
    y = mxq(f64(w1), 0, "e4m3").T @ xq
    pg = f64(mem).copy()
    pg[np.arange(H)[:, None], runs(slot, H)] = y
    z = pg[np.arange(H)[:, None], runs(r1, H)] - (f64(mem)[np.arange(H)[:, None], runs(r2, H)])
    out_0 = unpack_weight(w2_words, w2_scales).T @ mxq(z, 0, "e4m3")
    return (out_0,) + planes(out_0)

@@ -1,0 +1,190 @@
+from contextlib import ExitStack
+
+import concourse.mybir as mybir
+
+K, T, S, V, N, U, H = 512, 2048, 512, 1024, 512, 1024, 512
+FLOPS = 2 * K * H * S + 2 * H * N * V
+
+F32 = mybir.dt.float32
+BF16 = mybir.dt.bfloat16
+I32 = mybir.dt.int32
+U32 = mybir.dt.uint32
+U16 = mybir.dt.uint16
+U8 = mybir.dt.uint8
+FP8X4 = mybir.dt.float8_e4m3fn_x4
+SUB = mybir.AluOpType.subtract
+
+P = 128
+PACK = 4
+CH = 256
+NCH = V // CH
+
+
+def tile_picked_evictread_none_po_kernel(tc, x_words, x_scales, w1, mem, w2_words, w2_scales, offs, slot, r1, r2, out_0, out_1, out_2):
+    nc = tc.nc
+    with ExitStack() as ctx:
+        lists = ctx.enter_context(tc.tile_pool(name="lists", bufs=1))
+        keep = ctx.enter_context(tc.tile_pool(name="keep", bufs=1))
+        psum = ctx.enter_context(tc.psum_pool(name="psum", bufs=8))
+
+        def sb(shape, dtype, name, tag=None):
+            return keep.tile(shape, dtype, name=name, tag=tag or name, align_bytes=64)
+
+        offs_sb = lists.tile([P, S // 16], U16, name="offs_sb")
+        slot_sb = lists.tile([P, S // 16], U16, name="slot_sb")
+        r1_sb = lists.tile([P, V // 16], U16, name="r1_sb")
+        r2_sb = lists.tile([P, V // 16], U16, name="r2_sb")
+
+        xw = sb([P, T], U32, "xw")
+        xs = sb([P, T], U8, "xs")
+        w2w = sb([P, N], U32, "w2w")
+        w2s = sb([P, N], U8, "w2s")
+        old = [sb([P, U], F32, "old%d" % t) for t in range(PACK)]
+        page = [sb([P, U], F32, "page%d" % t) for t in range(PACK)]
+        w1raw = [sb([P, PACK, H // 2], F32, "w1raw%d" % h) for h in range(2)]
+        mem_t = mem.rearrange("(p t) u -> t p u", t=PACK)
+        w1_v = w1.rearrange("(p j) c -> p j c", j=PACK)
+
+        nc.vector.memset(xs[:].bitcast(I32), 0)
+        nc.vector.memset(w2s[:].bitcast(I32), 0)
+
+        def load_scales(eng, tile, rows):
+            for q in range(4):
+                eng.dma_start(out=tile[32 * q : 32 * q + 4, :].bitcast(I32), in_=rows[4 * q : 4 * q + 4, :].bitcast(I32))
+
+        nc.sync.dma_start(out=w2w[:].bitcast(I32), in_=w2_words[0].rearrange("p n t -> p (n t)").bitcast(I32))
+        nc.sync.dma_start(r2_sb[:], r2)
+        nc.sync.dma_start(out=old[0][:], in_=mem_t[0])
+        nc.sync.dma_start(offs_sb[:], offs)
+        nc.sync.dma_start(out=xw[:].bitcast(I32), in_=x_words[0].rearrange("p n t -> p (n t)").bitcast(I32))
+        load_scales(nc.scalar, xs, x_scales[0])
+        for h in range(2):
+            nc.sync.dma_start(out=w1raw[h][:], in_=w1_v[:, :, h * (H // 2) : (h + 1) * (H // 2)])
+        nc.sync.dma_start(out=old[1][:], in_=mem_t[1])
+        nc.sync.dma_start(slot_sb[:], slot)
+        nc.sync.dma_start(out=page[0][:], in_=mem_t[0])
+        nc.sync.dma_start(r1_sb[:], r1)
+        load_scales(nc.sync, w2s, w2_scales[0])
+        nc.sync.dma_start(out=page[1][:], in_=mem_t[1])
+        nc.sync.dma_start(out=page[2][:], in_=mem_t[2])
+        nc.sync.dma_start(out=old[2][:], in_=mem_t[2])
+        nc.sync.dma_start(out=old[3][:], in_=mem_t[3])
+        nc.sync.dma_start(out=page[3][:], in_=mem_t[3])
+
+        w2wd = sb([P, N], U32, "w2wd")
+        nc.vector.tensor_copy(out=w2wd[:].bitcast(I32).rearrange("p (t m) -> p m t", t=PACK), in_=w2w[:].bitcast(I32).rearrange("p (m t) -> p m t", t=PACK))
+
+        before = {}
+
+        def read_old(t, lo, n, tag=None):
+            tile = sb([P, n], F32, "before%d_%d" % (t, lo), tag)
+            nc.vector.tensor_copy(tile[:], old[t][:].indirect(r2_sb[:, lo // 16 : (lo + n) // 16]))
+            for c in range(lo // CH, (lo + n) // CH):
+                before[t, c] = tile[:, c * CH - lo : (c + 1) * CH - lo]
+
+        read_old(0, 0, 512)
+        read_old(0, 512, 512)
+
+        xg = sb([P, S], U32, "xg")
+        xgs = sb([P, S], U8, "xgs")
+        nc.vector.tensor_copy(xg[:], xw[:].indirect(offs_sb[:]))
+        nc.vector.tensor_copy(xgs[:], xs[:].indirect(offs_sb[:]))
+
+        w1g = sb([P, PACK * H], BF16, "w1g", "w1g")
+        for h in range(2):
+            nc.scalar.copy(
+                out=w1g[:].rearrange("p (t m j) -> p m t j", t=PACK, j=PACK)[:, 64 * h : 64 * (h + 1)],
+                in_=w1raw[h][:].rearrange("p j (m t) -> p m t j", t=PACK),
+            )
+        read_old(1, 0, 512)
+        w1q = sb([P, H], U32, "w1q")
+        w1s = sb([P, H], U8, "w1s")
+        nc.vector.quantize_mx(out=w1q[:].bitcast(FP8X4), scales=w1s[:], in_=w1g[:])
+        read_old(1, 512, 512, "w1g")
+
+        w2sd = sb([P, N], U8, "w2sd")
+        nc.vector.tensor_copy(out=w2sd[:].rearrange("p (t m) -> p t m", t=PACK), in_=w2s[:].rearrange("p (m t) -> p t m", t=PACK))
+
+        for t in range(PACK):
+            cols = slice(t * P, (t + 1) * P)
+            bank = psum.tile([P, S], F32, name="ybank%d" % t, tag="bank")
+            nc.tensor.matmul_mx(out=bank[:], lhsT=w1q[:, cols].bitcast(FP8X4), lhsT_scale=w1s[:, cols], rhs=xg[:].bitcast(FP8X4), rhs_scale=xgs[:], start=True, stop=True)
+            y = sb([P, S], F32, "y%d" % t, "z1" if t == PACK - 1 else None)
+            nc.scalar.copy(out=y[:], in_=bank[:])
+            nc.vector.tensor_copy(page[t][:].indirect(slot_sb[:]), y[:])
+
+        codes = sb([P, V], U32, "codes")
+        scales = sb([P, V], U8, "scales")
+        out_v = out_0.rearrange("(p t) v -> p t v", t=PACK)
+        words_v = out_1[0].rearrange("p n t -> p (n t)").bitcast(I32)
+        z = {}
+        zb = {}
+        ob = {}
+
+        def diff(c, t):
+            if t == 0:
+                z[c] = sb([P, PACK, CH], F32, "zf%d" % c, "z%d" % (c % 2))
+            if t >= 2:
+                read_old(t, c * CH, CH, "zb" if t == 2 else None)
+            nc.vector.tensor_tensor(z[c][:, t, :], page[t][:].indirect(r1_sb[:, c * CH // 16 : (c + 1) * CH // 16]), before[t, c], SUB)
+
+        def weave(c):
+            zb[c] = sb([P, CH, PACK], BF16, "zb%d" % c, "zb")
+            dst = zb[c][:].rearrange("p (c i) t -> p c t i", i=4)
+            src = z[c][:].rearrange("p t (c i) -> p c t i", i=4)
+            if c == NCH - 1:
+                nc.vector.tensor_copy(out=dst, in_=src)
+            else:
+                nc.scalar.copy(out=dst, in_=src)
+
+        def product(c):
+            zq = sb([P, CH], U32, "zq%d" % c)
+            zs = sb([P, CH], U8, "zs%d" % c)
+            nc.vector.quantize_mx(out=zq[:].bitcast(FP8X4), scales=zs[:], in_=zb[c][:].rearrange("p v t -> p (v t)"))
+            banks = []
+            for h in range(CH // P):
+                bank = psum.tile([P, PACK, P], F32, name="obank%d_%d" % (c, h), tag="bank")
+                vs = slice(h * P, (h + 1) * P)
+                for t in range(PACK):
+                    cols = slice(t * P, (t + 1) * P)
+                    nc.tensor.matmul_mx(out=bank[:, t, :], lhsT=w2wd[:, cols].bitcast(FP8X4), lhsT_scale=w2sd[:, cols], rhs=zq[:, vs].bitcast(FP8X4), rhs_scale=zs[:, vs], start=True, stop=True)
+                banks.append(bank)
+            ob[c] = sb([P, CH, PACK], BF16, "ob%d" % c, "z%d" % (c % 2))
+            last = c == NCH - 1
+            for h in range(CH // P):
+                copy = nc.vector.tensor_copy if last and h == 1 else nc.scalar.copy
+                copy(out=ob[c][:, h * P : (h + 1) * P, :], in_=banks[h][:].rearrange("p t v -> p v t"))
+            if last:
+                for h in range(CH // P):
+                    copy = nc.vector.tensor_copy if h == 1 else nc.scalar.copy
+                    of = sb([P, PACK, P], F32, "of%d_%d" % (c, h))
+                    copy(out=of[:], in_=banks[h][:])
+                    nc.sync.dma_start(out=out_v[:, :, c * CH + h * P : c * CH + (h + 1) * P], in_=of[:])
+            else:
+                of = sb([P, PACK, CH], F32, "of%d" % c)
+                for h in range(CH // P):
+                    nc.scalar.copy(out=of[:, :, h * P : (h + 1) * P], in_=banks[h][:])
+                nc.sync.dma_start(out=out_v[:, :, c * CH : (c + 1) * CH], in_=of[:])
+
+        def hand_on(c):
+            vs = slice(c * CH, (c + 1) * CH)
+            nc.vector.quantize_mx(out=codes[:, vs].bitcast(FP8X4), scales=scales[:, vs], in_=ob[c][:].rearrange("p v t -> p (v t)"))
+            nc.sync.dma_start(out=words_v[:, vs], in_=codes[:, vs].bitcast(I32))
+
+        for t in range(PACK):
+            diff(0, t)
+        for c in range(NCH):
+            weave(c)
+            if c >= 1:
+                hand_on(c - 1)
+            if c + 1 < NCH:
+                diff(c + 1, 0)
+                diff(c + 1, 1)
+            product(c)
+            if c + 1 < NCH:
+                diff(c + 1, 2)
+                diff(c + 1, 3)
+        hand_on(NCH - 1)
+        for q in range(4):
+            eng = nc.scalar if q % 2 else nc.sync
+            eng.dma_start(out=out_2[0][4 * q : 4 * q + 4, :].bitcast(I32), in_=scales[32 * q : 32 * q + 4, :].bitcast(I32))

@@ -25,6 +25,7 @@ def tile_picked_evictread_none_po_kernel(tc, x_words, x_scales, w1, mem, w2_word
     with ExitStack() as ctx:
         lists = ctx.enter_context(tc.tile_pool(name="lists", bufs=1))
         keep = ctx.enter_context(tc.tile_pool(name="keep", bufs=1))
+        reuse = ctx.enter_context(tc.tile_pool(name="reuse", bufs=1))
         psum = ctx.enter_context(tc.psum_pool(name="psum", bufs=8))
 
         def sb(shape, dtype, name, tag=None):
@@ -52,33 +53,30 @@ def tile_picked_evictread_none_po_kernel(tc, x_words, x_scales, w1, mem, w2_word
             for q in range(4):
                 eng.dma_start(out=tile[32 * q : 32 * q + 4, :].bitcast(I32), in_=rows[4 * q : 4 * q + 4, :].bitcast(I32))
 
-        nc.sync.dma_start(out=w2w[:].bitcast(I32), in_=w2_words[0].rearrange("p n t -> p (n t)").bitcast(I32))
         nc.sync.dma_start(r2_sb[:], r2)
         nc.sync.dma_start(out=old[0][:], in_=mem_t[0])
+        load_scales(nc.scalar, xs, x_scales[0])
         nc.sync.dma_start(offs_sb[:], offs)
         nc.sync.dma_start(out=xw[:].bitcast(I32), in_=x_words[0].rearrange("p n t -> p (n t)").bitcast(I32))
-        load_scales(nc.scalar, xs, x_scales[0])
-        for h in range(2):
-            nc.sync.dma_start(out=w1raw[h][:], in_=w1_v[:, :, h * (H // 2) : (h + 1) * (H // 2)])
+        nc.sync.dma_start(out=w1raw[0][:], in_=w1_v[:, :, : H // 2])
         nc.sync.dma_start(out=old[1][:], in_=mem_t[1])
-        nc.sync.dma_start(slot_sb[:], slot)
-        nc.sync.dma_start(out=page[0][:], in_=mem_t[0])
-        nc.sync.dma_start(r1_sb[:], r1)
+        nc.sync.dma_start(out=w1raw[1][:], in_=w1_v[:, :, H // 2 :])
+        nc.sync.dma_start(out=w2w[:].bitcast(I32), in_=w2_words[0].rearrange("p n t -> p (n t)").bitcast(I32))
         load_scales(nc.sync, w2s, w2_scales[0])
-        nc.sync.dma_start(out=page[1][:], in_=mem_t[1])
-        nc.sync.dma_start(out=page[2][:], in_=mem_t[2])
         nc.sync.dma_start(out=old[2][:], in_=mem_t[2])
+        nc.sync.dma_start(slot_sb[:], slot)
+        for t in range(PACK):
+            nc.sync.dma_start(out=page[t][:], in_=mem_t[t])
         nc.sync.dma_start(out=old[3][:], in_=mem_t[3])
-        nc.sync.dma_start(out=page[3][:], in_=mem_t[3])
-
-        w2wd = sb([P, N], U32, "w2wd")
-        nc.vector.tensor_copy(out=w2wd[:].bitcast(I32).rearrange("p (t m) -> p m t", t=PACK), in_=w2w[:].bitcast(I32).rearrange("p (m t) -> p m t", t=PACK))
+        nc.sync.dma_start(r1_sb[:], r1)
 
         before = {}
 
-        def read_old(t, lo, n, tag=None):
-            tile = sb([P, n], F32, "before%d_%d" % (t, lo), tag)
-            nc.vector.tensor_copy(tile[:], old[t][:].indirect(r2_sb[:, lo // 16 : (lo + n) // 16]))
+        def read_old(t, lo, n, tag=None, tile=None):
+            if tile is None:
+                fresh = sb([P, n], F32, "before%d_%d" % (t, lo), tag)
+                tile = fresh[:]
+            nc.vector.tensor_copy(tile, old[t][:].indirect(r2_sb[:, lo // 16 : (lo + n) // 16]))
             for c in range(lo // CH, (lo + n) // CH):
                 before[t, c] = tile[:, c * CH - lo : (c + 1) * CH - lo]
 
@@ -90,26 +88,30 @@ def tile_picked_evictread_none_po_kernel(tc, x_words, x_scales, w1, mem, w2_word
         nc.vector.tensor_copy(xg[:], xw[:].indirect(offs_sb[:]))
         nc.vector.tensor_copy(xgs[:], xs[:].indirect(offs_sb[:]))
 
-        w1g = sb([P, PACK * H], BF16, "w1g", "w1g")
+        w1g = reuse.tile([P, PACK * H], BF16, name="w1g", offset=0, align_bytes=64)
         for h in range(2):
             nc.scalar.copy(
                 out=w1g[:].rearrange("p (t m j) -> p m t j", t=PACK, j=PACK)[:, 64 * h : 64 * (h + 1)],
                 in_=w1raw[h][:].rearrange("p j (m t) -> p m t j", t=PACK),
             )
         read_old(1, 0, 512)
+        read_old(1, 512, 512)
         w1q = sb([P, H], U32, "w1q")
         w1s = sb([P, H], U8, "w1s")
         nc.vector.quantize_mx(out=w1q[:].bitcast(FP8X4), scales=w1s[:], in_=w1g[:])
-        read_old(1, 512, 512, "w1g")
 
-        w2sd = sb([P, N], U8, "w2sd")
+        w2wd = reuse.tile([P, N], U32, name="w2wd", offset=0, align_bytes=64)
+        w2sd = reuse.tile([P, N], U8, name="w2sd", offset=2048, align_bytes=64)
+        first2 = reuse.tile([P, CH], F32, name="first2", offset=2560, align_bytes=64)
+        nc.vector.tensor_copy(out=w2wd[:].bitcast(I32).rearrange("p (t m) -> p m t", t=PACK), in_=w2w[:].bitcast(I32).rearrange("p (m t) -> p m t", t=PACK))
         nc.vector.tensor_copy(out=w2sd[:].rearrange("p (t m) -> p t m", t=PACK), in_=w2s[:].rearrange("p (m t) -> p t m", t=PACK))
+        read_old(2, 0, CH, tile=first2[:])
 
         for t in range(PACK):
             cols = slice(t * P, (t + 1) * P)
             bank = psum.tile([P, S], F32, name="ybank%d" % t, tag="bank")
             nc.tensor.matmul_mx(out=bank[:], lhsT=w1q[:, cols].bitcast(FP8X4), lhsT_scale=w1s[:, cols], rhs=xg[:].bitcast(FP8X4), rhs_scale=xgs[:], start=True, stop=True)
-            y = sb([P, S], F32, "y%d" % t, "z1" if t == PACK - 1 else None)
+            y = sb([P, S], F32, "y%d" % t, None)
             nc.scalar.copy(out=y[:], in_=bank[:])
             nc.vector.tensor_copy(page[t][:].indirect(slot_sb[:]), y[:])
 
@@ -121,21 +123,25 @@ def tile_picked_evictread_none_po_kernel(tc, x_words, x_scales, w1, mem, w2_word
         zb = {}
         ob = {}
 
+        LAST = NCH - 1
+
         def diff(c, t):
             if t == 0:
                 z[c] = sb([P, PACK, CH], F32, "zf%d" % c, "z%d" % (c % 2))
-            if t >= 2:
-                read_old(t, c * CH, CH, "zb" if t == 2 else None)
+            if t >= 2 and (t, c) not in before:
+                read_old(t, c * CH, CH, "zb" if t == 2 else "z%d" % ((c + 1) % 2))
             nc.vector.tensor_tensor(z[c][:, t, :], page[t][:].indirect(r1_sb[:, c * CH // 16 : (c + 1) * CH // 16]), before[t, c], SUB)
 
         def weave(c):
             zb[c] = sb([P, CH, PACK], BF16, "zb%d" % c, "zb")
             dst = zb[c][:].rearrange("p (c i) t -> p c t i", i=4)
             src = z[c][:].rearrange("p t (c i) -> p c t i", i=4)
-            if c == NCH - 1:
-                nc.vector.tensor_copy(out=dst, in_=src)
-            else:
-                nc.scalar.copy(out=dst, in_=src)
+            nc.scalar.copy(out=dst, in_=src)
+
+        def multiply(bank, zq, zs):
+            for t in range(PACK):
+                cols = slice(t * P, (t + 1) * P)
+                nc.tensor.matmul_mx(out=bank[:, t, :], lhsT=w2wd[:, cols].bitcast(FP8X4), lhsT_scale=w2sd[:, cols], rhs=zq.bitcast(FP8X4), rhs_scale=zs, start=True, stop=True)
 
         def product(c):
             zq = sb([P, CH], U32, "zq%d" % c)
@@ -145,26 +151,40 @@ def tile_picked_evictread_none_po_kernel(tc, x_words, x_scales, w1, mem, w2_word
             for h in range(CH // P):
                 bank = psum.tile([P, PACK, P], F32, name="obank%d_%d" % (c, h), tag="bank")
                 vs = slice(h * P, (h + 1) * P)
-                for t in range(PACK):
-                    cols = slice(t * P, (t + 1) * P)
-                    nc.tensor.matmul_mx(out=bank[:, t, :], lhsT=w2wd[:, cols].bitcast(FP8X4), lhsT_scale=w2sd[:, cols], rhs=zq[:, vs].bitcast(FP8X4), rhs_scale=zs[:, vs], start=True, stop=True)
+                multiply(bank, zq[:, vs], zs[:, vs])
                 banks.append(bank)
-            ob[c] = sb([P, CH, PACK], BF16, "ob%d" % c, "z%d" % (c % 2))
-            last = c == NCH - 1
+            ob[c] = sb([P, CH, PACK], BF16, "ob%d" % c)
             for h in range(CH // P):
-                copy = nc.vector.tensor_copy if last and h == 1 else nc.scalar.copy
+                nc.scalar.copy(out=ob[c][:, h * P : (h + 1) * P, :], in_=banks[h][:].rearrange("p t v -> p v t"))
+            of = sb([P, PACK, CH], F32, "of%d" % c)
+            for h in range(CH // P):
+                nc.scalar.copy(out=of[:, :, h * P : (h + 1) * P], in_=banks[h][:])
+            nc.sync.dma_start(out=out_v[:, :, c * CH : (c + 1) * CH], in_=of[:])
+
+        def last_product():
+            c = LAST
+            halves = [sb([P, P, PACK], BF16, "zlast%d" % h) for h in range(2)]
+            for pair, copy in ((0, nc.scalar.copy), (1, nc.vector.tensor_copy)):
+                for h in range(2):
+                    dst = halves[h][:].rearrange("p (c i) t -> p c t i", i=4)
+                    src = z[c][:, :PACK, h * P : (h + 1) * P].rearrange("p t (c i) -> p c t i", i=4)
+                    copy(out=dst[:, :, 2 * pair : 2 * pair + 2, :], in_=src[:, :, 2 * pair : 2 * pair + 2, :])
+            banks = []
+            for h in range(2):
+                zq = sb([P, P], U32, "zqlast%d" % h)
+                zs = sb([P, P], U8, "zslast%d" % h)
+                nc.vector.quantize_mx(out=zq[:].bitcast(FP8X4), scales=zs[:], in_=halves[h][:].rearrange("p v t -> p (v t)"))
+                bank = psum.tile([P, PACK, P], F32, name="obank%d_%d" % (c, h), tag="bank")
+                multiply(bank, zq[:], zs[:])
+                banks.append(bank)
+            hand_on(c - 1)
+            ob[c] = sb([P, CH, PACK], BF16, "ob%d" % c)
+            for h, copy in ((0, nc.scalar.copy), (1, nc.vector.tensor_copy)):
                 copy(out=ob[c][:, h * P : (h + 1) * P, :], in_=banks[h][:].rearrange("p t v -> p v t"))
-            if last:
-                for h in range(CH // P):
-                    copy = nc.vector.tensor_copy if h == 1 else nc.scalar.copy
-                    of = sb([P, PACK, P], F32, "of%d_%d" % (c, h))
-                    copy(out=of[:], in_=banks[h][:])
-                    nc.sync.dma_start(out=out_v[:, :, c * CH + h * P : c * CH + (h + 1) * P], in_=of[:])
-            else:
-                of = sb([P, PACK, CH], F32, "of%d" % c)
-                for h in range(CH // P):
-                    nc.scalar.copy(out=of[:, :, h * P : (h + 1) * P], in_=banks[h][:])
-                nc.sync.dma_start(out=out_v[:, :, c * CH : (c + 1) * CH], in_=of[:])
+            for h in range(2):
+                of = sb([P, PACK, P], F32, "of%d_%d" % (c, h))
+                nc.scalar.copy(out=of[:], in_=banks[h][:])
+                nc.sync.dma_start(out=out_v[:, :, c * CH + h * P : c * CH + (h + 1) * P], in_=of[:])
 
         def hand_on(c):
             vs = slice(c * CH, (c + 1) * CH)
@@ -173,18 +193,17 @@ def tile_picked_evictread_none_po_kernel(tc, x_words, x_scales, w1, mem, w2_word
 
         for t in range(PACK):
             diff(0, t)
-        for c in range(NCH):
+        for c in range(LAST):
             weave(c)
+            diff(c + 1, 0)
+            diff(c + 1, 1)
             if c >= 1:
                 hand_on(c - 1)
-            if c + 1 < NCH:
-                diff(c + 1, 0)
-                diff(c + 1, 1)
             product(c)
-            if c + 1 < NCH:
-                diff(c + 1, 2)
-                diff(c + 1, 3)
-        hand_on(NCH - 1)
+            diff(c + 1, 2)
+            diff(c + 1, 3)
+        last_product()
+        hand_on(LAST)
         for q in range(4):
             eng = nc.scalar if q % 2 else nc.sync
             eng.dma_start(out=out_2[0][4 * q : 4 * q + 4, :].bitcast(I32), in_=scales[32 * q : 32 * q + 4, :].bitcast(I32))

@@ -12,12 +12,19 @@ U32 = mybir.dt.uint32
 U16 = mybir.dt.uint16
 U8 = mybir.dt.uint8
 FP8X4 = mybir.dt.float8_e4m3fn_x4
-SUB = mybir.AluOpType.subtract
+SUBTRACT = mybir.AluOpType.subtract
 
 P = 128
 PACK = 4
-CH = 256
-NCH = V // CH
+GROUP = 16
+QUADRANTS = 4
+BANKS = 8
+CHUNK = 256
+CHUNKS = V // CHUNK
+LAST = CHUNKS - 1
+HALVES = CHUNK // P
+EARLY = 2
+LINE = 4
 
 
 def tile_picked_evictread_none_po_kernel(tc, x_words, x_scales, w1, mem, w2_words, w2_scales, offs, slot, r1, r2, out_0, out_1, out_2):
@@ -26,62 +33,60 @@ def tile_picked_evictread_none_po_kernel(tc, x_words, x_scales, w1, mem, w2_word
         lists = ctx.enter_context(tc.tile_pool(name="lists", bufs=1))
         keep = ctx.enter_context(tc.tile_pool(name="keep", bufs=1))
         reuse = ctx.enter_context(tc.tile_pool(name="reuse", bufs=1))
-        psum = ctx.enter_context(tc.psum_pool(name="psum", bufs=8))
+        psum = ctx.enter_context(tc.psum_pool(name="psum", bufs=BANKS))
 
         def sb(shape, dtype, name, tag=None):
             return keep.tile(shape, dtype, name=name, tag=tag or name, align_bytes=64)
 
-        offs_sb = lists.tile([P, S // 16], U16, name="offs_sb")
-        slot_sb = lists.tile([P, S // 16], U16, name="slot_sb")
-        r1_sb = lists.tile([P, V // 16], U16, name="r1_sb")
-        r2_sb = lists.tile([P, V // 16], U16, name="r2_sb")
+        offs_sb = lists.tile([P, S // GROUP], U16, name="offs_sb")
+        slot_sb = lists.tile([P, S // GROUP], U16, name="slot_sb")
+        r1_sb = lists.tile([P, V // GROUP], U16, name="r1_sb")
+        r2_sb = lists.tile([P, V // GROUP], U16, name="r2_sb")
 
         xw = sb([P, T], U32, "xw")
         xs = sb([P, T], U8, "xs")
         w2w = sb([P, N], U32, "w2w")
         w2s = sb([P, N], U8, "w2s")
-        old = [sb([P, U], F32, "old%d" % t) for t in range(PACK)]
+        old = [sb([P, 2 * U if t < EARLY else U], F32, "old%d" % t) for t in range(PACK)]
         page = [sb([P, U], F32, "page%d" % t) for t in range(PACK)]
         w1raw = [sb([P, PACK, H // 2], F32, "w1raw%d" % h) for h in range(2)]
-        mem_t = mem.rearrange("(p t) u -> t p u", t=PACK)
-        w1_v = w1.rearrange("(p j) c -> p j c", j=PACK)
+        mem_planes = mem.rearrange("(p t) u -> t p u", t=PACK)
+        w1_rows = w1.rearrange("(p j) c -> p j c", j=PACK)
 
         nc.vector.memset(xs[:].bitcast(I32), 0)
         nc.vector.memset(w2s[:].bitcast(I32), 0)
 
-        def load_scales(eng, tile, rows):
-            for q in range(4):
-                eng.dma_start(out=tile[32 * q : 32 * q + 4, :].bitcast(I32), in_=rows[4 * q : 4 * q + 4, :].bitcast(I32))
+        def load_scales(engine, tile, rows):
+            for q in range(QUADRANTS):
+                engine.dma_start(out=tile[32 * q : 32 * q + 4, :].bitcast(I32), in_=rows[4 * q : 4 * q + 4, :].bitcast(I32))
 
         nc.sync.dma_start(r2_sb[:], r2)
-        nc.sync.dma_start(out=old[0][:], in_=mem_t[0])
+        nc.sync.dma_start(out=old[0][:, :U], in_=mem_planes[0])
         load_scales(nc.scalar, xs, x_scales[0])
+        nc.sync.dma_start(out=old[1][:, :U], in_=mem_planes[1])
         nc.sync.dma_start(offs_sb[:], offs)
         nc.sync.dma_start(out=xw[:].bitcast(I32), in_=x_words[0].rearrange("p n t -> p (n t)").bitcast(I32))
-        nc.sync.dma_start(out=w1raw[0][:], in_=w1_v[:, :, : H // 2])
-        nc.sync.dma_start(out=old[1][:], in_=mem_t[1])
-        nc.sync.dma_start(out=w1raw[1][:], in_=w1_v[:, :, H // 2 :])
+        for h in range(2):
+            nc.sync.dma_start(out=w1raw[h][:], in_=w1_rows[:, :, h * (H // 2) : (h + 1) * (H // 2)])
         nc.sync.dma_start(out=w2w[:].bitcast(I32), in_=w2_words[0].rearrange("p n t -> p (n t)").bitcast(I32))
         load_scales(nc.sync, w2s, w2_scales[0])
-        nc.sync.dma_start(out=old[2][:], in_=mem_t[2])
+        for t in range(EARLY, PACK):
+            nc.sync.dma_start(out=old[t][:], in_=mem_planes[t])
         nc.sync.dma_start(slot_sb[:], slot)
         for t in range(PACK):
-            nc.sync.dma_start(out=page[t][:], in_=mem_t[t])
-        nc.sync.dma_start(out=old[3][:], in_=mem_t[3])
+            nc.sync.dma_start(out=page[t][:], in_=mem_planes[t])
         nc.sync.dma_start(r1_sb[:], r1)
 
         before = {}
 
-        def read_old(t, lo, n, tag=None, tile=None):
-            if tile is None:
-                fresh = sb([P, n], F32, "before%d_%d" % (t, lo), tag)
-                tile = fresh[:]
-            nc.vector.tensor_copy(tile, old[t][:].indirect(r2_sb[:, lo // 16 : (lo + n) // 16]))
-            for c in range(lo // CH, (lo + n) // CH):
-                before[t, c] = tile[:, c * CH - lo : (c + 1) * CH - lo]
+        def read_old(t, lo, tile):
+            n = tile.shape[1]
+            nc.vector.tensor_copy(tile[:], old[t][:].indirect(r2_sb[:, lo // GROUP : (lo + n) // GROUP]))
+            for c in range(lo // CHUNK, (lo + n) // CHUNK):
+                before[t, c] = tile[:, c * CHUNK - lo : (c + 1) * CHUNK - lo]
 
-        read_old(0, 0, 512)
-        read_old(0, 512, 512)
+        for t in range(EARLY):
+            read_old(t, 0, sb([P, V], F32, "before%d_0" % t))
 
         xg = sb([P, S], U32, "xg")
         xgs = sb([P, S], U8, "xgs")
@@ -91,52 +96,52 @@ def tile_picked_evictread_none_po_kernel(tc, x_words, x_scales, w1, mem, w2_word
         w1g = reuse.tile([P, PACK * H], BF16, name="w1g", offset=0, align_bytes=64)
         for h in range(2):
             nc.scalar.copy(
-                out=w1g[:].rearrange("p (t m j) -> p m t j", t=PACK, j=PACK)[:, 64 * h : 64 * (h + 1)],
+                out=w1g[:].rearrange("p (t m j) -> p m t j", t=PACK, j=PACK)[:, h * (P // 2) : (h + 1) * (P // 2)],
                 in_=w1raw[h][:].rearrange("p j (m t) -> p m t j", t=PACK),
             )
-        read_old(1, 0, 512)
-        read_old(1, 512, 512)
+        w2wd = sb([P, N], U32, "w2wd")
+        nc.vector.tensor_copy(
+            out=w2wd[:].bitcast(I32).rearrange("p (t m) -> p m t", t=PACK),
+            in_=w2w[:].bitcast(I32).rearrange("p (m t) -> p m t", t=PACK),
+        )
         w1q = sb([P, H], U32, "w1q")
         w1s = sb([P, H], U8, "w1s")
         nc.vector.quantize_mx(out=w1q[:].bitcast(FP8X4), scales=w1s[:], in_=w1g[:])
 
-        w2wd = reuse.tile([P, N], U32, name="w2wd", offset=0, align_bytes=64)
-        w2sd = reuse.tile([P, N], U8, name="w2sd", offset=2048, align_bytes=64)
-        first2 = reuse.tile([P, CH], F32, name="first2", offset=2560, align_bytes=64)
-        nc.vector.tensor_copy(out=w2wd[:].bitcast(I32).rearrange("p (t m) -> p m t", t=PACK), in_=w2w[:].bitcast(I32).rearrange("p (m t) -> p m t", t=PACK))
-        nc.vector.tensor_copy(out=w2sd[:].rearrange("p (t m) -> p t m", t=PACK), in_=w2s[:].rearrange("p (m t) -> p t m", t=PACK))
-        read_old(2, 0, CH, tile=first2[:])
+        w2sd = reuse.tile([P, N], U8, name="w2sd", offset=0, align_bytes=64)
+        first2 = reuse.tile([P, CHUNK], F32, name="first2", offset=2 * N, align_bytes=64)
+        nc.vector.tensor_copy(out=w2sd[:].rearrange("p (t m) -> p m t", t=PACK), in_=w2s[:].rearrange("p (m t) -> p m t", t=PACK))
+        read_old(2, 0, first2)
+        read_old(3, 0, sb([P, CHUNK], F32, "before3_0", "z1"))
 
         for t in range(PACK):
             cols = slice(t * P, (t + 1) * P)
             bank = psum.tile([P, S], F32, name="ybank%d" % t, tag="bank")
             nc.tensor.matmul_mx(out=bank[:], lhsT=w1q[:, cols].bitcast(FP8X4), lhsT_scale=w1s[:, cols], rhs=xg[:].bitcast(FP8X4), rhs_scale=xgs[:], start=True, stop=True)
-            y = sb([P, S], F32, "y%d" % t, None)
+            y = sb([P, S], F32, "y%d" % t)
             nc.scalar.copy(out=y[:], in_=bank[:])
             nc.vector.tensor_copy(page[t][:].indirect(slot_sb[:]), y[:])
 
         codes = sb([P, V], U32, "codes")
         scales = sb([P, V], U8, "scales")
-        out_v = out_0.rearrange("(p t) v -> p t v", t=PACK)
-        words_v = out_1[0].rearrange("p n t -> p (n t)").bitcast(I32)
+        out_planes = out_0.rearrange("(p t) v -> p t v", t=PACK)
+        out_words = out_1[0].rearrange("p n t -> p (n t)").bitcast(I32)
         z = {}
         zb = {}
         ob = {}
 
-        LAST = NCH - 1
-
-        def diff(c, t):
+        def difference(c, t):
             if t == 0:
-                z[c] = sb([P, PACK, CH], F32, "zf%d" % c, "z%d" % (c % 2))
-            if t >= 2 and (t, c) not in before:
-                read_old(t, c * CH, CH, "zb" if t == 2 else "z%d" % ((c + 1) % 2))
-            nc.vector.tensor_tensor(z[c][:, t, :], page[t][:].indirect(r1_sb[:, c * CH // 16 : (c + 1) * CH // 16]), before[t, c], SUB)
+                z[c] = sb([P, PACK, CHUNK], F32, "zf%d" % c, "z%d" % (c % 2))
+            if (t, c) not in before:
+                tag = "zb" if t == 2 else "z%d" % ((c + 1) % 2)
+                read_old(t, c * CHUNK, sb([P, CHUNK], F32, "before%d_%d" % (t, c * CHUNK), tag))
+            picks = r1_sb[:, c * CHUNK // GROUP : (c + 1) * CHUNK // GROUP]
+            nc.vector.tensor_tensor(z[c][:, t, :], page[t][:].indirect(picks), before[t, c], SUBTRACT)
 
         def weave(c):
-            zb[c] = sb([P, CH, PACK], BF16, "zb%d" % c, "zb")
-            dst = zb[c][:].rearrange("p (c i) t -> p c t i", i=4)
-            src = z[c][:].rearrange("p t (c i) -> p c t i", i=4)
-            nc.scalar.copy(out=dst, in_=src)
+            zb[c] = sb([P, CHUNK, PACK], BF16, "zb%d" % c, "zb")
+            nc.scalar.copy(out=zb[c][:].rearrange("p (c i) t -> p c t i", i=LINE), in_=z[c][:].rearrange("p t (c i) -> p c t i", i=LINE))
 
         def multiply(bank, zq, zs):
             for t in range(PACK):
@@ -144,66 +149,67 @@ def tile_picked_evictread_none_po_kernel(tc, x_words, x_scales, w1, mem, w2_word
                 nc.tensor.matmul_mx(out=bank[:, t, :], lhsT=w2wd[:, cols].bitcast(FP8X4), lhsT_scale=w2sd[:, cols], rhs=zq.bitcast(FP8X4), rhs_scale=zs, start=True, stop=True)
 
         def product(c):
-            zq = sb([P, CH], U32, "zq%d" % c)
-            zs = sb([P, CH], U8, "zs%d" % c)
+            zq = sb([P, CHUNK], U32, "zq%d" % c)
+            zs = sb([P, CHUNK], U8, "zs%d" % c)
             nc.vector.quantize_mx(out=zq[:].bitcast(FP8X4), scales=zs[:], in_=zb[c][:].rearrange("p v t -> p (v t)"))
             banks = []
-            for h in range(CH // P):
+            for h in range(HALVES):
                 bank = psum.tile([P, PACK, P], F32, name="obank%d_%d" % (c, h), tag="bank")
                 vs = slice(h * P, (h + 1) * P)
                 multiply(bank, zq[:, vs], zs[:, vs])
                 banks.append(bank)
-            ob[c] = sb([P, CH, PACK], BF16, "ob%d" % c)
-            for h in range(CH // P):
+            ob[c] = sb([P, CHUNK, PACK], BF16, "ob%d" % c)
+            for h in range(HALVES):
                 nc.scalar.copy(out=ob[c][:, h * P : (h + 1) * P, :], in_=banks[h][:].rearrange("p t v -> p v t"))
-            of = sb([P, PACK, CH], F32, "of%d" % c)
-            for h in range(CH // P):
+            of = sb([P, PACK, CHUNK], F32, "of%d" % c)
+            for h in range(HALVES):
                 nc.scalar.copy(out=of[:, :, h * P : (h + 1) * P], in_=banks[h][:])
-            nc.sync.dma_start(out=out_v[:, :, c * CH : (c + 1) * CH], in_=of[:])
+            nc.sync.dma_start(out=out_planes[:, :, c * CHUNK : (c + 1) * CHUNK], in_=of[:])
+
+        def hand_on(c):
+            vs = slice(c * CHUNK, (c + 1) * CHUNK)
+            nc.vector.quantize_mx(out=codes[:, vs].bitcast(FP8X4), scales=scales[:, vs], in_=ob[c][:].rearrange("p v t -> p (v t)"))
+            nc.sync.dma_start(out=out_words[:, vs], in_=codes[:, vs].bitcast(I32))
 
         def last_product():
-            c = LAST
-            halves = [sb([P, P, PACK], BF16, "zlast%d" % h) for h in range(2)]
+            halves = [sb([P, P, PACK], BF16, "zlast%d" % h) for h in range(HALVES)]
             for pair, copy in ((0, nc.scalar.copy), (1, nc.vector.tensor_copy)):
-                for h in range(2):
-                    dst = halves[h][:].rearrange("p (c i) t -> p c t i", i=4)
-                    src = z[c][:, :PACK, h * P : (h + 1) * P].rearrange("p t (c i) -> p c t i", i=4)
-                    copy(out=dst[:, :, 2 * pair : 2 * pair + 2, :], in_=src[:, :, 2 * pair : 2 * pair + 2, :])
+                planes = slice(2 * pair, 2 * pair + 2)
+                for h in range(HALVES):
+                    dst = halves[h][:].rearrange("p (c i) t -> p c t i", i=LINE)
+                    src = z[LAST][:, :, h * P : (h + 1) * P].rearrange("p t (c i) -> p c t i", i=LINE)
+                    copy(out=dst[:, :, planes, :], in_=src[:, :, planes, :])
             banks = []
-            for h in range(2):
+            for h in range(HALVES):
                 zq = sb([P, P], U32, "zqlast%d" % h)
                 zs = sb([P, P], U8, "zslast%d" % h)
                 nc.vector.quantize_mx(out=zq[:].bitcast(FP8X4), scales=zs[:], in_=halves[h][:].rearrange("p v t -> p (v t)"))
-                bank = psum.tile([P, PACK, P], F32, name="obank%d_%d" % (c, h), tag="bank")
+                bank = psum.tile([P, PACK, P], F32, name="obank%d_%d" % (LAST, h), tag="bank")
                 multiply(bank, zq[:], zs[:])
                 banks.append(bank)
-            hand_on(c - 1)
-            ob[c] = sb([P, CH, PACK], BF16, "ob%d" % c)
+            hand_on(LAST - 1)
+            ob[LAST] = sb([P, CHUNK, PACK], BF16, "ob%d" % LAST)
             for h, copy in ((0, nc.scalar.copy), (1, nc.vector.tensor_copy)):
-                copy(out=ob[c][:, h * P : (h + 1) * P, :], in_=banks[h][:].rearrange("p t v -> p v t"))
-            for h in range(2):
-                of = sb([P, PACK, P], F32, "of%d_%d" % (c, h))
+                copy(out=ob[LAST][:, h * P : (h + 1) * P, :], in_=banks[h][:].rearrange("p t v -> p v t"))
+            for h in range(HALVES):
+                of = sb([P, PACK, P], F32, "of%d_%d" % (LAST, h))
                 nc.scalar.copy(out=of[:], in_=banks[h][:])
-                nc.sync.dma_start(out=out_v[:, :, c * CH + h * P : c * CH + (h + 1) * P], in_=of[:])
-
-        def hand_on(c):
-            vs = slice(c * CH, (c + 1) * CH)
-            nc.vector.quantize_mx(out=codes[:, vs].bitcast(FP8X4), scales=scales[:, vs], in_=ob[c][:].rearrange("p v t -> p (v t)"))
-            nc.sync.dma_start(out=words_v[:, vs], in_=codes[:, vs].bitcast(I32))
+                nc.sync.dma_start(out=out_planes[:, :, LAST * CHUNK + h * P : LAST * CHUNK + (h + 1) * P], in_=of[:])
 
         for t in range(PACK):
-            diff(0, t)
+            difference(0, t)
         for c in range(LAST):
             weave(c)
-            diff(c + 1, 0)
-            diff(c + 1, 1)
+            difference(c + 1, 0)
+            difference(c + 1, 1)
             if c >= 1:
                 hand_on(c - 1)
             product(c)
-            diff(c + 1, 2)
-            diff(c + 1, 3)
+            difference(c + 1, 2)
+            difference(c + 1, 3)
         last_product()
         hand_on(LAST)
-        for q in range(4):
-            eng = nc.scalar if q % 2 else nc.sync
-            eng.dma_start(out=out_2[0][4 * q : 4 * q + 4, :].bitcast(I32), in_=scales[32 * q : 32 * q + 4, :].bitcast(I32))
+
+        for q in range(QUADRANTS):
+            engine = nc.scalar if q % 2 else nc.sync
+            engine.dma_start(out=out_2[0][4 * q : 4 * q + 4, :].bitcast(I32), in_=scales[32 * q : 32 * q + 4, :].bitcast(I32))

from contextlib import ExitStack

import concourse.mybir as mybir

K, T, S, V, N, U, H = 512, 2048, 512, 1024, 512, 1024, 512
FLOPS = 2 * K * H * S + 2 * H * N * V

F32 = mybir.dt.float32
BF16 = mybir.dt.bfloat16
I32 = mybir.dt.int32
U32 = mybir.dt.uint32
U16 = mybir.dt.uint16
U8 = mybir.dt.uint8
FP8X4 = mybir.dt.float8_e4m3fn_x4
SUBTRACT = mybir.AluOpType.subtract

P = 128
PACK = 4
GROUP = 16
QUADRANTS = 4
BANKS = 8
CHUNK = 256
CHUNKS = V // CHUNK
LAST = CHUNKS - 1
HALVES = CHUNK // P
EARLY = 2
LINE = 4


def tile_picked_evictread_none_po_kernel(tc, x_words, x_scales, w1, mem, w2_words, w2_scales, offs, slot, r1, r2, out_0, out_1, out_2):
    nc = tc.nc
    with ExitStack() as ctx:
        lists = ctx.enter_context(tc.tile_pool(name="lists", bufs=1))
        keep = ctx.enter_context(tc.tile_pool(name="keep", bufs=1))
        reuse = ctx.enter_context(tc.tile_pool(name="reuse", bufs=1))
        psum = ctx.enter_context(tc.psum_pool(name="psum", bufs=BANKS))

        def sb(shape, dtype, name, tag=None):
            return keep.tile(shape, dtype, name=name, tag=tag or name, align_bytes=64)

        offs_sb = lists.tile([P, S // GROUP], U16, name="offs_sb")
        slot_sb = lists.tile([P, S // GROUP], U16, name="slot_sb")
        r1_sb = lists.tile([P, V // GROUP], U16, name="r1_sb")
        r2_sb = lists.tile([P, V // GROUP], U16, name="r2_sb")

        xw = sb([P, T], U32, "xw")
        xs = sb([P, T], U8, "xs")
        w2w = sb([P, N], U32, "w2w")
        w2s = sb([P, N], U8, "w2s")
        old = [sb([P, 2 * U if t < EARLY else U], F32, "old%d" % t) for t in range(PACK)]
        page = [sb([P, U], F32, "page%d" % t) for t in range(PACK)]
        w1raw = [sb([P, PACK, H // 2], F32, "w1raw%d" % h) for h in range(2)]
        mem_planes = mem.rearrange("(p t) u -> t p u", t=PACK)
        w1_rows = w1.rearrange("(p j) c -> p j c", j=PACK)

        nc.vector.memset(xs[:].bitcast(I32), 0)
        nc.vector.memset(w2s[:].bitcast(I32), 0)

        def load_scales(engine, tile, rows):
            for q in range(QUADRANTS):
                engine.dma_start(out=tile[32 * q : 32 * q + 4, :].bitcast(I32), in_=rows[4 * q : 4 * q + 4, :].bitcast(I32))

        nc.sync.dma_start(r2_sb[:], r2)
        nc.sync.dma_start(out=old[0][:, :U], in_=mem_planes[0])
        load_scales(nc.scalar, xs, x_scales[0])
        nc.sync.dma_start(out=old[1][:, :U], in_=mem_planes[1])
        nc.sync.dma_start(offs_sb[:], offs)
        nc.sync.dma_start(out=xw[:].bitcast(I32), in_=x_words[0].rearrange("p n t -> p (n t)").bitcast(I32))
        for h in range(2):
            nc.sync.dma_start(out=w1raw[h][:], in_=w1_rows[:, :, h * (H // 2) : (h + 1) * (H // 2)])
        nc.sync.dma_start(out=w2w[:].bitcast(I32), in_=w2_words[0].rearrange("p n t -> p (n t)").bitcast(I32))
        load_scales(nc.sync, w2s, w2_scales[0])
        for t in range(EARLY, PACK):
            nc.sync.dma_start(out=old[t][:], in_=mem_planes[t])
        nc.sync.dma_start(slot_sb[:], slot)
        for t in range(PACK):
            nc.sync.dma_start(out=page[t][:], in_=mem_planes[t])
        nc.sync.dma_start(r1_sb[:], r1)

        before = {}

        def read_old(t, lo, tile):
            n = tile.shape[1]
            nc.vector.tensor_copy(tile[:], old[t][:].indirect(r2_sb[:, lo // GROUP : (lo + n) // GROUP]))
            for c in range(lo // CHUNK, (lo + n) // CHUNK):
                before[t, c] = tile[:, c * CHUNK - lo : (c + 1) * CHUNK - lo]

        for t in range(EARLY):
            read_old(t, 0, sb([P, V], F32, "before%d_0" % t))

        xg = sb([P, S], U32, "xg")
        xgs = sb([P, S], U8, "xgs")
        nc.vector.tensor_copy(xg[:], xw[:].indirect(offs_sb[:]))
        nc.vector.tensor_copy(xgs[:], xs[:].indirect(offs_sb[:]))

        w1g = reuse.tile([P, PACK * H], BF16, name="w1g", offset=0, align_bytes=64)
        for h in range(2):
            nc.scalar.copy(
                out=w1g[:].rearrange("p (t m j) -> p m t j", t=PACK, j=PACK)[:, h * (P // 2) : (h + 1) * (P // 2)],
                in_=w1raw[h][:].rearrange("p j (m t) -> p m t j", t=PACK),
            )
        w2wd = sb([P, N], U32, "w2wd")
        nc.vector.tensor_copy(
            out=w2wd[:].bitcast(I32).rearrange("p (t m) -> p m t", t=PACK),
            in_=w2w[:].bitcast(I32).rearrange("p (m t) -> p m t", t=PACK),
        )
        w1q = sb([P, H], U32, "w1q")
        w1s = sb([P, H], U8, "w1s")
        nc.vector.quantize_mx(out=w1q[:].bitcast(FP8X4), scales=w1s[:], in_=w1g[:])

        w2sd = reuse.tile([P, N], U8, name="w2sd", offset=0, align_bytes=64)
        first2 = reuse.tile([P, CHUNK], F32, name="first2", offset=2 * N, align_bytes=64)
        nc.vector.tensor_copy(out=w2sd[:].rearrange("p (t m) -> p m t", t=PACK), in_=w2s[:].rearrange("p (m t) -> p m t", t=PACK))
        read_old(2, 0, first2)
        read_old(3, 0, sb([P, CHUNK], F32, "before3_0", "z1"))

        for t in range(PACK):
            cols = slice(t * P, (t + 1) * P)
            bank = psum.tile([P, S], F32, name="ybank%d" % t, tag="bank")
            nc.tensor.matmul_mx(out=bank[:], lhsT=w1q[:, cols].bitcast(FP8X4), lhsT_scale=w1s[:, cols], rhs=xg[:].bitcast(FP8X4), rhs_scale=xgs[:], start=True, stop=True)
            y = sb([P, S], F32, "y%d" % t)
            nc.scalar.copy(out=y[:], in_=bank[:])
            nc.vector.tensor_copy(page[t][:].indirect(slot_sb[:]), y[:])

        codes = sb([P, V], U32, "codes")
        scales = sb([P, V], U8, "scales")
        out_planes = out_0.rearrange("(p t) v -> p t v", t=PACK)
        out_words = out_1[0].rearrange("p n t -> p (n t)").bitcast(I32)
        z = {}
        zb = {}
        ob = {}

        def difference(c, t):
            if t == 0:
                z[c] = sb([P, PACK, CHUNK], F32, "zf%d" % c, "z%d" % (c % 2))
            if (t, c) not in before:
                tag = "zb" if t == 2 else "z%d" % ((c + 1) % 2)
                read_old(t, c * CHUNK, sb([P, CHUNK], F32, "before%d_%d" % (t, c * CHUNK), tag))
            picks = r1_sb[:, c * CHUNK // GROUP : (c + 1) * CHUNK // GROUP]
            nc.vector.tensor_tensor(z[c][:, t, :], page[t][:].indirect(picks), before[t, c], SUBTRACT)

        def weave(c):
            zb[c] = sb([P, CHUNK, PACK], BF16, "zb%d" % c, "zb")
            nc.scalar.copy(out=zb[c][:].rearrange("p (c i) t -> p c t i", i=LINE), in_=z[c][:].rearrange("p t (c i) -> p c t i", i=LINE))

        def multiply(bank, zq, zs):
            for t in range(PACK):
                cols = slice(t * P, (t + 1) * P)
                nc.tensor.matmul_mx(out=bank[:, t, :], lhsT=w2wd[:, cols].bitcast(FP8X4), lhsT_scale=w2sd[:, cols], rhs=zq.bitcast(FP8X4), rhs_scale=zs, start=True, stop=True)

        def product(c):
            zq = sb([P, CHUNK], U32, "zq%d" % c)
            zs = sb([P, CHUNK], U8, "zs%d" % c)
            nc.vector.quantize_mx(out=zq[:].bitcast(FP8X4), scales=zs[:], in_=zb[c][:].rearrange("p v t -> p (v t)"))
            banks = []
            for h in range(HALVES):
                bank = psum.tile([P, PACK, P], F32, name="obank%d_%d" % (c, h), tag="bank")
                vs = slice(h * P, (h + 1) * P)
                multiply(bank, zq[:, vs], zs[:, vs])
                banks.append(bank)
            ob[c] = sb([P, CHUNK, PACK], BF16, "ob%d" % c)
            for h in range(HALVES):
                nc.scalar.copy(out=ob[c][:, h * P : (h + 1) * P, :], in_=banks[h][:].rearrange("p t v -> p v t"))
            of = sb([P, PACK, CHUNK], F32, "of%d" % c)
            for h in range(HALVES):
                nc.scalar.copy(out=of[:, :, h * P : (h + 1) * P], in_=banks[h][:])
            nc.sync.dma_start(out=out_planes[:, :, c * CHUNK : (c + 1) * CHUNK], in_=of[:])

        def hand_on(c):
            vs = slice(c * CHUNK, (c + 1) * CHUNK)
            nc.vector.quantize_mx(out=codes[:, vs].bitcast(FP8X4), scales=scales[:, vs], in_=ob[c][:].rearrange("p v t -> p (v t)"))
            nc.sync.dma_start(out=out_words[:, vs], in_=codes[:, vs].bitcast(I32))

        def last_product():
            halves = [sb([P, P, PACK], BF16, "zlast%d" % h) for h in range(HALVES)]
            for pair, copy in ((0, nc.scalar.copy), (1, nc.vector.tensor_copy)):
                planes = slice(2 * pair, 2 * pair + 2)
                for h in range(HALVES):
                    dst = halves[h][:].rearrange("p (c i) t -> p c t i", i=LINE)
                    src = z[LAST][:, :, h * P : (h + 1) * P].rearrange("p t (c i) -> p c t i", i=LINE)
                    copy(out=dst[:, :, planes, :], in_=src[:, :, planes, :])
            banks = []
            for h in range(HALVES):
                zq = sb([P, P], U32, "zqlast%d" % h)
                zs = sb([P, P], U8, "zslast%d" % h)
                nc.vector.quantize_mx(out=zq[:].bitcast(FP8X4), scales=zs[:], in_=halves[h][:].rearrange("p v t -> p (v t)"))
                bank = psum.tile([P, PACK, P], F32, name="obank%d_%d" % (LAST, h), tag="bank")
                multiply(bank, zq[:], zs[:])
                banks.append(bank)
            hand_on(LAST - 1)
            ob[LAST] = sb([P, CHUNK, PACK], BF16, "ob%d" % LAST)
            for h, copy in ((0, nc.scalar.copy), (1, nc.vector.tensor_copy)):
                copy(out=ob[LAST][:, h * P : (h + 1) * P, :], in_=banks[h][:].rearrange("p t v -> p v t"))
            for h in range(HALVES):
                of = sb([P, PACK, P], F32, "of%d_%d" % (LAST, h))
                nc.scalar.copy(out=of[:], in_=banks[h][:])
                nc.sync.dma_start(out=out_planes[:, :, LAST * CHUNK + h * P : LAST * CHUNK + (h + 1) * P], in_=of[:])

        for t in range(PACK):
            difference(0, t)
        for c in range(LAST):
            weave(c)
            difference(c + 1, 0)
            difference(c + 1, 1)
            if c >= 1:
                hand_on(c - 1)
            product(c)
            difference(c + 1, 2)
            difference(c + 1, 3)
        last_product()
        hand_on(LAST)

        for q in range(QUADRANTS):
            engine = nc.scalar if q % 2 else nc.sync
            engine.dma_start(out=out_2[0][4 * q : 4 * q + 4, :].bitcast(I32), in_=scales[32 * q : 32 * q + 4, :].bitcast(I32))
